import numpy as np
import ml_dtypes


def mxq(x, axis, fmt="e4m3"):
    dtype, down = {"e4m3": (ml_dtypes.float8_e4m3fn, 7), "e5m2": (ml_dtypes.float8_e5m2, 14)}[fmt]
    v = np.moveaxis(np.asarray(x, np.float32).astype(ml_dtypes.bfloat16).astype(np.float64), axis, -1)
    blocks = v.reshape(v.shape[:-1] + (-1, 32))
    amax = np.abs(blocks).max(-1, keepdims=True)
    byte = np.maximum(np.where(amax > 0, np.frexp(amax)[1] - 1 + 127, 0) - down, 1)
    scale = np.exp2(byte - 127.0)
    codes = (blocks / scale).astype(np.float32).astype(dtype).astype(np.float64)
    return np.moveaxis((codes * scale).reshape(v.shape), -1, axis)


WIDE = False


def mx_kscale(k):
    if not WIDE:
        return np.ones(k)
    levels = np.array([10, -10, 5, -5, 0])
    if k % 512:
        return np.exp2(np.random.permutation(np.resize(levels, k // 32))).repeat(32)
    a = np.empty((k // 512, 16))
    for p in range(k // 512):
        a[p, :8] = np.random.permutation(np.resize(levels, 8))
        for g in range(8):
            far = levels[np.abs(levels - a[p, g]) >= 10]
            a[p, g + 8] = far[np.random.randint(len(far))]
    return np.exp2(a.ravel()).repeat(32)


def f64(x):
    return np.asarray(x).astype(np.float64)


def striped(idx):
    return np.tile(np.asarray(idx).reshape(-1, 16).T, (8, 1)).astype(np.uint16)


def unstriped(offs):
    return offs[:16].T.reshape(-1).astype(np.int64)


def striped8(idx):
    return np.asarray(idx).reshape(8, -1, 16).transpose(0, 2, 1).reshape(128, -1).astype(np.uint16)


def unstriped8(offs):
    return offs.reshape(8, 16, -1).transpose(0, 2, 1).reshape(8, -1).astype(np.int64)


def pick8(x, idx, run):
    r = np.arange(len(x))
    return x[r[:, None], idx[r % (8 * run) // run]]


E2M1 = np.array([0.0, 0.5, 1.0, 1.5, 2.0, 3.0, 4.0, 6.0, -0.0, -0.5, -1.0, -1.5, -2.0, -3.0, -4.0, -6.0])


def pack_weight(w, fmt):
    k, n = w.shape
    w = f64(np.asarray(w, np.float32).astype(ml_dtypes.bfloat16)).reshape(k // 32, 32, n)
    amax = np.abs(w).max(1)
    if fmt == "e4m3":
        byte = np.frexp(amax)[1] - 1 + 127 - 7
    else:
        mant, ex = np.frexp(amax / 6.0)
        byte = np.where(mant > 0.5, ex, ex - 1) + 127
    byte = np.clip(np.where(amax > 0, byte, 1), 1, 254)
    scaled = (w * np.exp2(127.0 - byte)[:, None, :]).reshape(k, n).astype(np.float32)
    by_word = np.ascontiguousarray(scaled.reshape(k // 512, 128, 4, n).transpose(0, 1, 3, 2))
    if fmt == "e4m3":
        words = by_word.astype(ml_dtypes.float8_e4m3fn).view(np.uint8)
    else:
        c = by_word.astype(ml_dtypes.float4_e2m1fn).view(np.uint8) & 0xF
        words = (c[..., 0::2] | (c[..., 1::2] << 4)).reshape(k // 512, 128, 2 * n)
    return np.ascontiguousarray(words), np.ascontiguousarray(byte.astype(np.uint8).reshape(k // 512, 16, n))


def unpack_weight(words, scales, fmt):
    g, _, n = scales.shape
    words = np.ascontiguousarray(words).reshape(g, 128, n, -1)
    if fmt == "e4m3":
        vals = words.view(ml_dtypes.float8_e4m3fn).astype(np.float64)
    else:
        nib = np.empty((g, 128, n, 4), np.uint8)
        nib[..., 0::2] = words & 0xF
        nib[..., 1::2] = words >> 4
        vals = E2M1[nib]
    vals = vals * np.repeat(np.exp2(scales.astype(np.float64) - 127.0), 8, axis=1)[..., None]
    return vals.transpose(0, 1, 3, 2).reshape(g * 512, n)


K, J, R, T, U, Z, M, O, C, N, S = 512, 256, 512, 512, 512, 512, 1024, 128, 512, 256, 512


def setup_inputs():
    n = np.random.standard_normal
    idx = np.stack([np.random.permutation(T)[:J] for _ in range(8)])
    idx2 = np.stack([np.random.permutation(U)[:J] for _ in range(8)])
    idx3 = np.random.permutation(M)[:J]
    idx4 = np.stack([np.random.permutation(C)[:J] for _ in range(8)])
    idx5 = np.stack([np.random.permutation(C)[:J] for _ in range(8)])
    idx6 = np.stack([np.random.permutation(J)[:O] for _ in range(8)])
    idx7 = np.stack([np.random.permutation(S)[:N] for _ in range(8)])
    fk = mx_kscale(K)
    fr = mx_kscale(R)
    fz = mx_kscale(Z)
    wp = pack_weight(n((K, R)) * 1 / np.sqrt(K) / fk[:, None] * fr, "e4m3")
    xop = pack_weight(n((Z, M)) / fz[:, None], "e4m3")
    w2p = pack_weight(n((Z, R)) * 1 / np.sqrt(Z) * fz[:, None] * fr, "e2m1")
    return {
        "ta": (np.random.randint(-7, 8, (K, T)).astype(np.float64)).astype(np.float32),
        "tb": (np.random.randint(-7, 8, (K, U)).astype(np.float64)).astype(np.float32),
        "ga": ((np.random.randint(10, 25, (K, 1)) / 64.0) * fk[:, None]).astype(np.float32),
        "gb": ((np.random.randint(4, 13, (K, 1)) / 64.0) * fk[:, None]).astype(np.float32),
        "w_words": wp[0],
        "w_scales": wp[1],
        "xo_words": xop[0],
        "xo_scales": xop[1],
        "w2_words": w2p[0],
        "w2_scales": w2p[1],
        "sa": (np.random.uniform(0.5, 1.6, (R, 1))).astype(np.float32),
        "sb": (np.random.uniform(0.5, 1.6, (R, 1))).astype(np.float32),
        "va": (np.random.randint(-7, 8, (R, S)).astype(np.float64)).astype(np.float32),
        "ea": ((np.random.randint(8, 25, (R, 1)) / 1024.0) / fr[:, None]).astype(np.float32),
        "offs": striped8(idx),
        "offs2": striped8(idx2),
        "offs3": striped(idx3),
        "offs4": striped8(idx4),
        "offs5": striped8(idx5),
        "offs6": striped8(idx6),
        "offs7": striped8(idx7),
    }


def reference(ta, tb, ga, gb, w_words, w_scales, xo_words, xo_scales, w2_words, w2_scales, sa, sb, va, ea, offs, offs2, offs3, offs4, offs5, offs6, offs7):
    idx = unstriped8(offs)
    idx2 = unstriped8(offs2)
    idx3 = unstriped(offs3)
    idx4 = unstriped8(offs4)
    idx5 = unstriped8(offs5)
    idx6 = unstriped8(offs6)
    idx7 = unstriped8(offs7)
    wu = unpack_weight(w_words, w_scales, "e4m3")
    xou = unpack_weight(xo_words, xo_scales, "e4m3")
    w2u = unpack_weight(w2_words, w2_scales, "e2m1")
    xc = pick8(f64(ta), idx, 64) * f64(ga) + pick8(f64(tb), idx2, 64) * f64(gb)
    xcq = mxq(xc, 0, "e4m3")
    a = wu.T @ xcq
    xoidx3g = xou[:, idx3]
    b = w2u.T @ xoidx3g
    pw = np.zeros((R, C))
    pw[np.arange(R)[:, None], idx4[np.arange(R) % 512 // 64]] = a
    g1 = np.maximum(pick8(pw, idx5, 64) * f64(sa), b)
    hid = pick8(g1, idx6, 64) * f64(sb)
    vc = pick8(f64(va), idx7, 64) * f64(ea)
    vcq = mxq(vc, 0, "e4m3")
    hidq = mxq(hid, 0, "e4m3")
    y = vcq.T @ hidq
    return y

@@ -1,0 +1,224 @@
+from contextlib import ExitStack
+
+import concourse.mybir as mybir
+
+F32 = mybir.dt.float32
+BF16 = mybir.dt.bfloat16
+I32 = mybir.dt.int32
+U32 = mybir.dt.uint32
+U16 = mybir.dt.uint16
+U8 = mybir.dt.uint8
+FP8X4 = mybir.dt.float8_e4m3fn_x4
+FP4X4 = mybir.dt.float4_e2m1fn_x4
+COPY = mybir.ActivationFunctionType.Copy
+ADD = mybir.AluOpType.add
+MAX = mybir.AluOpType.max
+
+P = 128
+PACK = 4
+QUADS = 4
+K, J, R, T, M, O, C, N = 512, 256, 512, 512, 1024, 128, 512, 256
+FLOPS = 2 * K * R * J + 2 * K * R * J + 2 * R * N * O
+
+
+def tile_picked_twobooks_plain_two_answered_codes_plain_kernel(
+    tc, ta, tb, ga, gb, w_words, w_scales, xo_words, xo_scales, w2_words, w2_scales,
+    sa, sb, va, ea, offs, offs2, offs3, offs4, offs5, offs6, offs7, out,
+):
+    nc = tc.nc
+    with ExitStack() as ctx:
+        lists = ctx.enter_context(tc.tile_pool(name="lists", bufs=1))
+        keep = ctx.enter_context(tc.tile_pool(name="keep", bufs=1))
+        reuse = ctx.enter_context(tc.tile_pool(name="reuse", bufs=1))
+        early = ctx.enter_context(tc.tile_pool(name="early", bufs=1))
+        psum = ctx.enter_context(tc.psum_pool(name="psum", bufs=1))
+
+        def load_list(src, name):
+            tile = lists.tile([P, src.shape[1]], U16, name=name)
+            nc.sync.dma_start(tile[:], src)
+            return tile
+
+        def load_factor(src, name, queue, tag=None):
+            tile = keep.tile([P, PACK], F32, name=name, tag=tag or name, align_bytes=64)
+            queue.dma_start(out=tile[:], in_=src.rearrange("(p t) o -> p (t o)", t=PACK))
+            return tile
+
+        def load_plane(src, t, name):
+            tile = keep.tile([P, T], F32, name=name, align_bytes=64)
+            nc.sync.dma_start(out=tile[:], in_=src.rearrange("(p t) c -> p t c", t=PACK)[:, t, :])
+            return tile
+
+        def load_scale_rows(dst, src):
+            nc.sync.dma_start(out=dst, in_=src[0].bitcast(I32).rearrange("(q r) c -> r q c", r=QUADS))
+
+        def load_words(src, name):
+            tile = keep.tile([P, src.shape[1]], I32, name=name)
+            nc.sync.dma_start(out=tile[:], in_=src)
+            return tile
+
+        def spread_scale_rows(dst, stage):
+            rows = stage.shape[0]
+            for q in range(QUADS):
+                nc.vector.tensor_copy(out=dst[32 * q : 32 * q + rows, :].bitcast(I32), in_=stage[:, q, :])
+
+        def interleave(copy, dst, src):
+            copy(out=dst.rearrange("p (c i) t -> p c t i", i=4), in_=src.rearrange("p t (c i) -> p c t i", i=4))
+
+        def dealt(ap):
+            return ap.rearrange("p (t m) -> p m t", t=PACK)
+
+        def plain(ap):
+            return ap.rearrange("p (m t) -> p m t", t=PACK)
+
+        ww_stage = keep.tile([32, QUADS, R // 4], I32, name="ww_stage")
+        nc.vector.memset(ww_stage[:], 0)
+        xo_stage = keep.tile([QUADS, QUADS, M // 4], I32, name="xo_stage")
+        list_a = load_list(offs, "list_a")
+        ta_rows = [load_plane(ta, 0, "ta0")]
+        ga_col = load_factor(ga, "ga_col", nc.scalar)
+        list_b = load_list(offs2, "list_b")
+        gb_col = load_factor(gb, "gb_col", nc.scalar)
+        tb_rows = [load_plane(tb, 0, "tb0")]
+        ta_rows.append(load_plane(ta, 1, "ta1"))
+        tb_rows.append(load_plane(tb, 1, "tb1"))
+        ta_rows.append(load_plane(ta, 2, "ta2"))
+        load_scale_rows(xo_stage[:], xo_scales)
+        tb_rows.append(load_plane(tb, 2, "tb2"))
+        list_xo = load_list(offs3, "list_xo")
+        load_scale_rows(ww_stage[0:QUADS], w2_scales)
+        load_scale_rows(ww_stage[QUADS : 2 * QUADS], w_scales)
+        ta_rows.append(load_plane(ta, 3, "ta3"))
+        tb_rows.append(load_plane(tb, 3, "tb3"))
+        w_raw = load_words(w_words[0].rearrange("p n t -> p (n t)").bitcast(I32), "w_raw")
+        xo_raw = reuse.tile([P, M], I32, name="xo_raw", offset=0)
+        nc.sync.dma_start(out=xo_raw[:], in_=xo_words[0].rearrange("p n t -> p (n t)").bitcast(I32))
+        list_put = load_list(offs4, "list_put")
+        w2_raw = load_words(w2_words[0].bitcast(I32), "w2_raw")
+        list_va = load_list(offs7, "list_va")
+        va_rows = [load_plane(va, t, "va%d" % t) for t in range(PACK)]
+        list_board = load_list(offs5, "list_board")
+        list_slot = load_list(offs6, "list_slot")
+        ea_col = load_factor(ea, "ea_col", nc.gpsimd, tag="va4")
+        sa_col = load_factor(sa, "sa_col", nc.gpsimd, tag="sa_then_hid")
+        sb_col = load_factor(sb, "sb_col", nc.gpsimd)
+
+        def cleared_board(t, tag):
+            board = keep.tile([P, C], F32, name="board%d" % t, tag=tag)
+            nc.vector.memset(board[:], 0.0)
+            return board
+
+        boards = [cleared_board(t, "board%d" % t) for t in range(PACK)]
+
+        xo_spread = early.tile([P, M], U8, name="xo_spread", offset=0)
+        nc.vector.memset(xo_spread[:].bitcast(I32), 0)
+        spread_scale_rows(xo_spread, xo_stage)
+        xo_sc = keep.tile([P, J], U8, name="xo_sc", align_bytes=64)
+        nc.vector.tensor_copy(out=xo_sc[:], in_=xo_spread[:].indirect(list_xo[:]))
+        ww_spread = early.tile([P, R], U8, name="ww_spread", offset=M)
+        spread_scale_rows(ww_spread, ww_stage)
+        ww_sc = keep.tile([P, R], U8, name="ww_sc", align_bytes=64)
+        nc.vector.tensor_copy(out=dealt(ww_sc[:]), in_=plain(ww_spread[:]))
+
+        xa = keep.tile([P, PACK, J], F32, name="xa")
+        xb = keep.tile([P, PACK, J], F32, name="xb")
+        xc = early.tile([P, J, PACK], BF16, name="xc", offset=0, align_bytes=64)
+
+        def add_pair(u, cols):
+            nc.vector.tensor_tensor(
+                out=xc[:, cols, 2 * u : 2 * u + 2],
+                in0=xa[:, 2 * u : 2 * u + 2, cols].rearrange("p t j -> p j t"),
+                in1=xb[:, 2 * u : 2 * u + 2, cols].rearrange("p t j -> p j t"),
+                op=ADD,
+            )
+
+        for t in range(PACK):
+            nc.scalar.activation(out=xa[:, t, :], in_=ta_rows[t][:].indirect(list_a[:]), func=COPY, scale=ga_col[:, t : t + 1])
+            if t < PACK - 1:
+                nc.scalar.activation(out=xb[:, t, :], in_=tb_rows[t][:].indirect(list_b[:]), func=COPY, scale=gb_col[:, t : t + 1])
+            if t == 1:
+                add_pair(0, slice(0, J))
+        for h in range(2):
+            cols = slice(h * J // 2, (h + 1) * J // 2)
+            nc.scalar.activation(
+                out=xb[:, PACK - 1, cols],
+                in_=tb_rows[PACK - 1][:].indirect(list_b[:, h * J // 32 : (h + 1) * J // 32]),
+                func=COPY,
+                scale=gb_col[:, PACK - 1 : PACK],
+            )
+            add_pair(1, cols)
+
+        w_codes = keep.tile([P, R], U32, name="w_codes", align_bytes=64)
+        nc.scalar.copy(out=dealt(w_codes[:]), in_=plain(w_raw[:].bitcast(U32)))
+        w2_codes = keep.tile([P, 2 * R], U8, name="w2_codes", align_bytes=64)
+        nc.scalar.copy(out=dealt(w2_codes[:].bitcast(U16)), in_=plain(w2_raw[:].bitcast(U16)))
+
+        xc_codes = keep.tile([P, J], U32, name="xc_codes", tag="chain", align_bytes=64)
+        xc_sc = keep.tile([P, J], U8, name="xc_sc", align_bytes=64)
+        nc.vector.quantize_mx(out=xc_codes[:].bitcast(FP8X4), scales=xc_sc[:], in_=xc[:].rearrange("p j t -> p (j t)"))
+
+        xo_codes = keep.tile([P, J], U32, name="xo_codes", align_bytes=64)
+        nc.vector.tensor_copy(out=xo_codes[:], in_=xo_raw[:].bitcast(U32).indirect(list_xo[:]))
+
+
+        a_rows = reuse.tile([P, PACK, J], F32, name="a_rows", offset=0)
+        for t in range(PACK):
+            cols = slice(t * P, (t + 1) * P)
+            a_bank = psum.tile([P, J], F32, name="a_bank%d" % t)
+            nc.tensor.matmul_mx(
+                out=a_bank[:], lhsT=w_codes[:, cols].bitcast(FP8X4), lhsT_scale=ww_sc[QUADS:P, cols],
+                rhs=xc_codes[:].bitcast(FP8X4), rhs_scale=xc_sc[:], start=True, stop=True,
+            )
+            nc.scalar.copy(out=a_rows[:, t, :], in_=a_bank[:])
+            nc.vector.tensor_copy(out=boards[t][:].indirect(list_put[:]), in_=a_rows[:, t, :])
+
+        b_banks = [psum.tile([P, 2, J], F32, name="b_bank%d" % u) for u in range(2)]
+        for t in range(PACK):
+            nc.tensor.matmul_mx(
+                out=b_banks[t // 2][:, t % 2, :],
+                lhsT=w2_codes[:, 2 * t * P : 2 * (t + 1) * P].bitcast(FP4X4), lhsT_scale=ww_sc[:, t * P : (t + 1) * P],
+                rhs=xo_codes[:].bitcast(FP8X4), rhs_scale=xo_sc[:], start=True, stop=True,
+            )
+
+        vc_rows = keep.tile([P, PACK, N], BF16, name="vc_rows", tag="chain", align_bytes=64)
+        for t in range(PACK):
+            nc.scalar.activation(out=vc_rows[:, t, :], in_=va_rows[t][:].indirect(list_va[:]), func=COPY, scale=ea_col[:, t : t + 1])
+        vc_lo = keep.tile([P, P, PACK], BF16, name="vc_lo", align_bytes=64)
+        interleave(nc.scalar.copy, vc_lo[:], vc_rows[:, :, 0:P])
+
+        answers = []
+        for t in range(PACK):
+            read = keep.tile([P, J], F32, name="read%d" % t, tag="va%d" % (t + 1), align_bytes=64)
+            nc.scalar.activation(out=read[:], in_=boards[t][:].indirect(list_board[:]), func=COPY, scale=sa_col[:, t : t + 1])
+            answer = reuse.tile([P, J], F32, name="answer%d" % t, offset=4 * J * t)
+            nc.vector.tensor_tensor(out=answer[:], in0=read[:], in1=b_banks[t // 2][:, t % 2, :], op=MAX)
+            answers.append(answer)
+        vc_hi = keep.tile([P, P, PACK], BF16, name="vc_hi", tag="va1", align_bytes=64)
+        interleave(nc.vector.tensor_copy, vc_hi[:], vc_rows[:, :, P:N])
+        vc_codes = keep.tile([P, N], U32, name="vc_codes", align_bytes=64)
+        vc_sc = keep.tile([P, N], U8, name="vc_sc", tag="va2", align_bytes=64)
+        for h, half in enumerate((vc_lo, vc_hi)):
+            cols = slice(h * P, (h + 1) * P)
+            nc.vector.quantize_mx(out=vc_codes[:, cols].bitcast(FP8X4), scales=vc_sc[:, cols], in_=half[:].rearrange("p n t -> p (n t)"))
+        hid_rows = keep.tile([P, PACK, O], BF16, name="hid_rows", tag="sa_then_hid", align_bytes=64)
+        for t in range(PACK):
+            nc.scalar.activation(out=hid_rows[:, t, :], in_=answers[t][:].indirect(list_slot[:]), func=COPY, scale=sb_col[:, t : t + 1])
+        hid = keep.tile([P, O, PACK], BF16, name="hid", align_bytes=64)
+        interleave(nc.vector.tensor_copy, hid[:], hid_rows[:])
+        hid_codes = keep.tile([P, O], U32, name="hid_codes", align_bytes=64)
+        hid_sc = keep.tile([P, O], U8, name="hid_sc", align_bytes=64)
+        nc.vector.quantize_mx(out=hid_codes[:].bitcast(FP8X4), scales=hid_sc[:], in_=hid[:].rearrange("p o t -> p (o t)"))
+
+        for h in range(2):
+            cols = slice(h * P, (h + 1) * P)
+            y_bank = psum.tile([P, O], F32, name="y_bank%d" % h)
+            nc.tensor.matmul_mx(
+                out=y_bank[:], lhsT=vc_codes[:, cols].bitcast(FP8X4), lhsT_scale=vc_sc[:, cols],
+                rhs=hid_codes[:].bitcast(FP8X4), rhs_scale=hid_sc[:], start=True, stop=True,
+            )
+            y = keep.tile([P, O], F32, name="y%d" % h)
+            if h == 0:
+                nc.vector.tensor_copy(out=y[:], in_=y_bank[:])
+                nc.sync.dma_start(out=out[cols, :], in_=y[:])
+            else:
+                nc.scalar.copy(out=y[:], in_=y_bank[:])
+                nc.scalar.dma_start(out=out[cols, :], in_=y[:])

@@ -70,37 +70,40 @@ def tile_picked_twobooks_plain_two_answered_codes_plain_kernel(
         def plain(ap):
             return ap.rearrange("p (m t) -> p m t", t=PACK)
 
+        warm = keep.tile([P, 2], F32, name="warm")
+        nc.vector.memset(warm[:, 0:1], 0.0)
+        nc.scalar.activation(out=warm[:, 1:2], in_=warm[:, 0:1], func=COPY)
         ww_stage = keep.tile([32, QUADS, R // 4], I32, name="ww_stage")
         nc.vector.memset(ww_stage[:], 0)
-        xo_stage = keep.tile([QUADS, QUADS, M // 4], I32, name="xo_stage")
+        xo_rows = early.tile([P, M], U8, name="xo_rows", offset=0)
+        nc.vector.memset(xo_rows[:].bitcast(I32), 0)
         list_a = load_list(offs, "list_a")
-        ta_rows = [load_plane(ta, 0, "ta0")]
         ga_col = load_factor(ga, "ga_col", nc.scalar)
-        list_b = load_list(offs2, "list_b")
-        gb_col = load_factor(gb, "gb_col", nc.scalar)
-        tb_rows = [load_plane(tb, 0, "tb0")]
-        ta_rows.append(load_plane(ta, 1, "ta1"))
-        tb_rows.append(load_plane(tb, 1, "tb1"))
-        ta_rows.append(load_plane(ta, 2, "ta2"))
-        load_scale_rows(xo_stage[:], xo_scales)
-        tb_rows.append(load_plane(tb, 2, "tb2"))
+        ta_rows = [load_plane(ta, 0, "ta0")]
         list_xo = load_list(offs3, "list_xo")
+        ta_rows.extend(load_plane(ta, t, "ta%d" % t) for t in range(1, PACK))
+        tb_rows = [load_plane(tb, 0, "tb0")]
+        list_b = load_list(offs2, "list_b")
+        nc.sync.dma_start(out=xo_rows[0:P:8, :].bitcast(I32), in_=xo_scales[0].bitcast(I32))
         load_scale_rows(ww_stage[0:QUADS], w2_scales)
         load_scale_rows(ww_stage[QUADS : 2 * QUADS], w_scales)
-        ta_rows.append(load_plane(ta, 3, "ta3"))
+        tb_rows.append(load_plane(tb, 1, "tb1"))
+        tb_rows.append(load_plane(tb, 2, "tb2"))
         tb_rows.append(load_plane(tb, 3, "tb3"))
         w_raw = load_words(w_words[0].rearrange("p n t -> p (n t)").bitcast(I32), "w_raw")
-        xo_raw = reuse.tile([P, M], I32, name="xo_raw", offset=0)
-        nc.sync.dma_start(out=xo_raw[:], in_=xo_words[0].rearrange("p n t -> p (n t)").bitcast(I32))
-        list_put = load_list(offs4, "list_put")
         w2_raw = load_words(w2_words[0].bitcast(I32), "w2_raw")
+        va_rows = [load_plane(va, 0, "va0")]
         list_va = load_list(offs7, "list_va")
-        va_rows = [load_plane(va, t, "va%d" % t) for t in range(PACK)]
+        xo_raw = load_words(xo_words[0].rearrange("p n t -> p (n t)").bitcast(I32), "xo_raw")
+        va_rows.append(load_plane(va, 1, "va1"))
+        list_put = load_list(offs4, "list_put")
+        va_rows.extend(load_plane(va, t, "va%d" % t) for t in range(2, PACK))
         list_board = load_list(offs5, "list_board")
+        sa_col = load_factor(sa, "sa_col", nc.sync, tag="sa_then_hid")
         list_slot = load_list(offs6, "list_slot")
+        sb_col = load_factor(sb, "sb_col", nc.sync)
+        gb_col = load_factor(gb, "gb_col", nc.gpsimd)
         ea_col = load_factor(ea, "ea_col", nc.gpsimd, tag="va4")
-        sa_col = load_factor(sa, "sa_col", nc.gpsimd, tag="sa_then_hid")
-        sb_col = load_factor(sb, "sb_col", nc.gpsimd)
 
         def cleared_board(t, tag):
             board = keep.tile([P, C], F32, name="board%d" % t, tag=tag)
@@ -109,15 +112,16 @@ def tile_picked_twobooks_plain_two_answered_codes_plain_kernel(
 
         boards = [cleared_board(t, "board%d" % t) for t in range(PACK)]
 
-        xo_spread = early.tile([P, M], U8, name="xo_spread", offset=0)
-        nc.vector.memset(xo_spread[:].bitcast(I32), 0)
-        spread_scale_rows(xo_spread, xo_stage)
+        xo_picked = keep.tile([P, J], U8, name="xo_picked")
+        nc.vector.tensor_copy(out=xo_picked[:], in_=xo_rows[:].indirect(list_xo[:]))
         xo_sc = keep.tile([P, J], U8, name="xo_sc", align_bytes=64)
-        nc.vector.tensor_copy(out=xo_sc[:], in_=xo_spread[:].indirect(list_xo[:]))
+        nc.vector.memset(xo_sc[:].bitcast(I32), 0)
+        for r in range(QUADS):
+            nc.sync.dma_start(out=xo_sc[r:P:32, :].bitcast(I32), in_=xo_picked[8 * r : P : 32, :].bitcast(I32))
         ww_spread = early.tile([P, R], U8, name="ww_spread", offset=M)
         spread_scale_rows(ww_spread, ww_stage)
         ww_sc = keep.tile([P, R], U8, name="ww_sc", align_bytes=64)
-        nc.vector.tensor_copy(out=dealt(ww_sc[:]), in_=plain(ww_spread[:]))
+        nc.vector.tensor_copy(out=ww_sc[:].rearrange("p (t m) -> p t m", t=PACK), in_=ww_spread[:].rearrange("p (m t) -> p t m", t=PACK))
 
         xa = keep.tile([P, PACK, J], F32, name="xa")
         xb = keep.tile([P, PACK, J], F32, name="xb")
@@ -133,10 +137,11 @@ def tile_picked_twobooks_plain_two_answered_codes_plain_kernel(
 
         for t in range(PACK):
             nc.scalar.activation(out=xa[:, t, :], in_=ta_rows[t][:].indirect(list_a[:]), func=COPY, scale=ga_col[:, t : t + 1])
-            if t < PACK - 1:
-                nc.scalar.activation(out=xb[:, t, :], in_=tb_rows[t][:].indirect(list_b[:]), func=COPY, scale=gb_col[:, t : t + 1])
-            if t == 1:
-                add_pair(0, slice(0, J))
+        for t in range(PACK - 1):
+            nc.scalar.activation(out=xb[:, t, :], in_=tb_rows[t][:].indirect(list_b[:]), func=COPY, scale=gb_col[:, t : t + 1])
+        add_pair(0, slice(0, J))
+        w_codes = keep.tile([P, R], I32, name="w_codes", align_bytes=64)
+        nc.vector.tensor_copy(out=dealt(w_codes[:]), in_=plain(w_raw[:]))
         for h in range(2):
             cols = slice(h * J // 2, (h + 1) * J // 2)
             nc.scalar.activation(
@@ -147,12 +152,13 @@ def tile_picked_twobooks_plain_two_answered_codes_plain_kernel(
             )
             add_pair(1, cols)
 
-        w_codes = keep.tile([P, R], U32, name="w_codes", align_bytes=64)
-        nc.scalar.copy(out=dealt(w_codes[:]), in_=plain(w_raw[:].bitcast(U32)))
         w2_codes = keep.tile([P, 2 * R], U8, name="w2_codes", align_bytes=64)
-        nc.scalar.copy(out=dealt(w2_codes[:].bitcast(U16)), in_=plain(w2_raw[:].bitcast(U16)))
+        nc.scalar.copy(
+            out=w2_codes[:].bitcast(U16).rearrange("p (t m) -> p t m", t=PACK),
+            in_=w2_raw[:].bitcast(U16).rearrange("p (m t) -> p t m", t=PACK),
+        )
 
-        xc_codes = keep.tile([P, J], U32, name="xc_codes", tag="chain", align_bytes=64)
+        xc_codes = keep.tile([P, J], U32, name="xc_codes", align_bytes=64)
         xc_sc = keep.tile([P, J], U8, name="xc_sc", align_bytes=64)
         nc.vector.quantize_mx(out=xc_codes[:].bitcast(FP8X4), scales=xc_sc[:], in_=xc[:].rearrange("p j t -> p (j t)"))
 
@@ -179,9 +185,10 @@ def tile_picked_twobooks_plain_two_answered_codes_plain_kernel(
                 rhs=xo_codes[:].bitcast(FP8X4), rhs_scale=xo_sc[:], start=True, stop=True,
             )
 
-        vc_rows = keep.tile([P, PACK, N], BF16, name="vc_rows", tag="chain", align_bytes=64)
+        vc_rows = keep.tile([P, PACK, N], BF16, name="vc_rows")
         for t in range(PACK):
             nc.scalar.activation(out=vc_rows[:, t, :], in_=va_rows[t][:].indirect(list_va[:]), func=COPY, scale=ea_col[:, t : t + 1])
+
         vc_lo = keep.tile([P, P, PACK], BF16, name="vc_lo", align_bytes=64)
         interleave(nc.scalar.copy, vc_lo[:], vc_rows[:, :, 0:P])
 
@@ -203,7 +210,9 @@ def tile_picked_twobooks_plain_two_answered_codes_plain_kernel(
         for t in range(PACK):
             nc.scalar.activation(out=hid_rows[:, t, :], in_=answers[t][:].indirect(list_slot[:]), func=COPY, scale=sb_col[:, t : t + 1])
         hid = keep.tile([P, O, PACK], BF16, name="hid", align_bytes=64)
-        interleave(nc.vector.tensor_copy, hid[:], hid_rows[:])
+        for u in range(2):
+            pair = slice(2 * u, 2 * u + 2)
+            nc.vector.tensor_copy(out=hid[:, :, pair], in_=hid_rows[:, pair, :].rearrange("p t o -> p o t"))
         hid_codes = keep.tile([P, O], U32, name="hid_codes", align_bytes=64)
         hid_sc = keep.tile([P, O], U8, name="hid_sc", align_bytes=64)
         nc.vector.quantize_mx(out=hid_codes[:].bitcast(FP8X4), scales=hid_sc[:], in_=hid[:].rearrange("p o t -> p (o t)"))

@@ -48,18 +48,20 @@ def tile_picked_twobooks_plain_two_answered_codes_plain_kernel(
             nc.sync.dma_start(out=tile[:], in_=src.rearrange("(p t) c -> p t c", t=PACK)[:, t, :])
             return tile
 
-        def load_scale_rows(dst, src):
-            nc.sync.dma_start(out=dst, in_=src[0].bitcast(I32).rearrange("(q r) c -> r q c", r=QUADS))
-
         def load_words(src, name):
             tile = keep.tile([P, src.shape[1]], I32, name=name)
             nc.sync.dma_start(out=tile[:], in_=src)
             return tile
 
-        def spread_scale_rows(dst, stage):
-            rows = stage.shape[0]
-            for q in range(QUADS):
-                nc.vector.tensor_copy(out=dst[32 * q : 32 * q + rows, :].bitcast(I32), in_=stage[:, q, :])
+        def place_scale_rows(src, name):
+            plane = keep.tile([P, src.shape[1]], U8, name=name, align_bytes=64)
+            nc.vector.memset(plane[:].bitcast(I32), 0)
+            for r in range(QUADS):
+                nc.sync.dma_start(out=plane[r:P:32, :].bitcast(I32), in_=src[8 * r : P : 32, :].bitcast(I32))
+            return plane
+
+        def deal_bytes(dst, src):
+            nc.vector.tensor_copy(out=dst[:].rearrange("p (t m) -> p t m", t=PACK), in_=src[:].rearrange("p (m t) -> p t m", t=PACK))
 
         def interleave(copy, dst, src):
             copy(out=dst.rearrange("p (c i) t -> p c t i", i=4), in_=src.rearrange("p t (c i) -> p c t i", i=4))
@@ -70,40 +72,36 @@ def tile_picked_twobooks_plain_two_answered_codes_plain_kernel(
         def plain(ap):
             return ap.rearrange("p (m t) -> p m t", t=PACK)
 
-        warm = keep.tile([P, 2], F32, name="warm")
-        nc.vector.memset(warm[:, 0:1], 0.0)
-        nc.scalar.activation(out=warm[:, 1:2], in_=warm[:, 0:1], func=COPY)
-        ww_stage = keep.tile([32, QUADS, R // 4], I32, name="ww_stage")
-        nc.vector.memset(ww_stage[:], 0)
         xo_rows = early.tile([P, M], U8, name="xo_rows", offset=0)
         nc.vector.memset(xo_rows[:].bitcast(I32), 0)
+        w2_rows = early.tile([P, R], U8, name="w2_rows", offset=M)
+        nc.vector.memset(w2_rows[:].bitcast(I32), 0)
+        w_stage = keep.tile([QUADS, QUADS, R // 4], I32, name="w_stage")
+        ta_rows = [load_plane(ta, 0, "ta0")]
         list_a = load_list(offs, "list_a")
         ga_col = load_factor(ga, "ga_col", nc.scalar)
-        ta_rows = [load_plane(ta, 0, "ta0")]
+        gb_col = load_factor(gb, "gb_col", nc.scalar)
+        nc.sync.dma_start(out=w_stage[:], in_=w_scales[0].bitcast(I32).rearrange("(q r) c -> r q c", r=QUADS))
+        ta_rows.append(load_plane(ta, 1, "ta1"))
         list_xo = load_list(offs3, "list_xo")
-        ta_rows.extend(load_plane(ta, t, "ta%d" % t) for t in range(1, PACK))
-        tb_rows = [load_plane(tb, 0, "tb0")]
-        list_b = load_list(offs2, "list_b")
+        ta_rows.append(load_plane(ta, 2, "ta2"))
         nc.sync.dma_start(out=xo_rows[0:P:8, :].bitcast(I32), in_=xo_scales[0].bitcast(I32))
-        load_scale_rows(ww_stage[0:QUADS], w2_scales)
-        load_scale_rows(ww_stage[QUADS : 2 * QUADS], w_scales)
-        tb_rows.append(load_plane(tb, 1, "tb1"))
-        tb_rows.append(load_plane(tb, 2, "tb2"))
-        tb_rows.append(load_plane(tb, 3, "tb3"))
+        nc.sync.dma_start(out=w2_rows[0:P:8, :].bitcast(I32), in_=w2_scales[0].bitcast(I32))
+        ta_rows.append(load_plane(ta, 3, "ta3"))
+        list_b = load_list(offs2, "list_b")
+        tb_rows = [load_plane(tb, t, "tb%d" % t) for t in range(PACK)]
         w_raw = load_words(w_words[0].rearrange("p n t -> p (n t)").bitcast(I32), "w_raw")
-        w2_raw = load_words(w2_words[0].bitcast(I32), "w2_raw")
-        va_rows = [load_plane(va, 0, "va0")]
-        list_va = load_list(offs7, "list_va")
         xo_raw = load_words(xo_words[0].rearrange("p n t -> p (n t)").bitcast(I32), "xo_raw")
-        va_rows.append(load_plane(va, 1, "va1"))
         list_put = load_list(offs4, "list_put")
-        va_rows.extend(load_plane(va, t, "va%d" % t) for t in range(2, PACK))
+        w2_raw = load_words(w2_words[0].bitcast(I32), "w2_raw")
+        list_va = load_list(offs7, "list_va")
+        ea_col = load_factor(ea, "ea_col", nc.sync, tag="va4")
+        va_rows = [load_plane(va, t, "va%d" % t) for t in range(2)]
         list_board = load_list(offs5, "list_board")
         sa_col = load_factor(sa, "sa_col", nc.sync, tag="sa_then_hid")
+        va_rows.extend(load_plane(va, t, "va%d" % t) for t in range(2, PACK))
         list_slot = load_list(offs6, "list_slot")
         sb_col = load_factor(sb, "sb_col", nc.sync)
-        gb_col = load_factor(gb, "gb_col", nc.gpsimd)
-        ea_col = load_factor(ea, "ea_col", nc.gpsimd, tag="va4")
 
         def cleared_board(t, tag):
             board = keep.tile([P, C], F32, name="board%d" % t, tag=tag)
@@ -112,16 +110,18 @@ def tile_picked_twobooks_plain_two_answered_codes_plain_kernel(
 
         boards = [cleared_board(t, "board%d" % t) for t in range(PACK)]
 
+        w_spread = early.tile([P, R], U8, name="w_spread", offset=M + R)
+        nc.vector.memset(w_spread[:].bitcast(I32), 0)
+        for q in range(QUADS):
+            nc.vector.tensor_copy(out=w_spread[32 * q : 32 * q + QUADS, :].bitcast(I32), in_=w_stage[:, q, :])
+        w_sc = keep.tile([P, R], U8, name="w_sc", align_bytes=64)
+        deal_bytes(w_sc, w_spread)
         xo_picked = keep.tile([P, J], U8, name="xo_picked")
         nc.vector.tensor_copy(out=xo_picked[:], in_=xo_rows[:].indirect(list_xo[:]))
-        xo_sc = keep.tile([P, J], U8, name="xo_sc", align_bytes=64)
-        nc.vector.memset(xo_sc[:].bitcast(I32), 0)
-        for r in range(QUADS):
-            nc.sync.dma_start(out=xo_sc[r:P:32, :].bitcast(I32), in_=xo_picked[8 * r : P : 32, :].bitcast(I32))
-        ww_spread = early.tile([P, R], U8, name="ww_spread", offset=M)
-        spread_scale_rows(ww_spread, ww_stage)
-        ww_sc = keep.tile([P, R], U8, name="ww_sc", align_bytes=64)
-        nc.vector.tensor_copy(out=ww_sc[:].rearrange("p (t m) -> p t m", t=PACK), in_=ww_spread[:].rearrange("p (m t) -> p t m", t=PACK))
+        xo_sc = place_scale_rows(xo_picked, "xo_sc")
+        w2_dealt = keep.tile([P, R], U8, name="w2_dealt")
+        deal_bytes(w2_dealt, w2_rows)
+        w2_sc = place_scale_rows(w2_dealt, "w2_sc")
 
         xa = keep.tile([P, PACK, J], F32, name="xa")
         xb = keep.tile([P, PACK, J], F32, name="xb")
@@ -140,8 +140,6 @@ def tile_picked_twobooks_plain_two_answered_codes_plain_kernel(
         for t in range(PACK - 1):
             nc.scalar.activation(out=xb[:, t, :], in_=tb_rows[t][:].indirect(list_b[:]), func=COPY, scale=gb_col[:, t : t + 1])
         add_pair(0, slice(0, J))
-        w_codes = keep.tile([P, R], I32, name="w_codes", align_bytes=64)
-        nc.vector.tensor_copy(out=dealt(w_codes[:]), in_=plain(w_raw[:]))
         for h in range(2):
             cols = slice(h * J // 2, (h + 1) * J // 2)
             nc.scalar.activation(
@@ -152,36 +150,51 @@ def tile_picked_twobooks_plain_two_answered_codes_plain_kernel(
             )
             add_pair(1, cols)
 
-        w2_codes = keep.tile([P, 2 * R], U8, name="w2_codes", align_bytes=64)
-        nc.scalar.copy(
-            out=w2_codes[:].bitcast(U16).rearrange("p (t m) -> p t m", t=PACK),
-            in_=w2_raw[:].bitcast(U16).rearrange("p (m t) -> p t m", t=PACK),
-        )
+        w_codes = keep.tile([P, R], U32, name="w_codes", align_bytes=64)
+        nc.scalar.copy(out=dealt(w_codes[:]), in_=plain(w_raw[:].bitcast(U32)))
 
         xc_codes = keep.tile([P, J], U32, name="xc_codes", align_bytes=64)
         xc_sc = keep.tile([P, J], U8, name="xc_sc", align_bytes=64)
-        nc.vector.quantize_mx(out=xc_codes[:].bitcast(FP8X4), scales=xc_sc[:], in_=xc[:].rearrange("p j t -> p (j t)"))
+        for h in range(2):
+            cols = slice(h * J // 2, (h + 1) * J // 2)
+            nc.vector.quantize_mx(out=xc_codes[:, cols].bitcast(FP8X4), scales=xc_sc[:, cols], in_=xc[:, cols, :].rearrange("p j t -> p (j t)"))
 
         xo_codes = keep.tile([P, J], U32, name="xo_codes", align_bytes=64)
         nc.vector.tensor_copy(out=xo_codes[:], in_=xo_raw[:].bitcast(U32).indirect(list_xo[:]))
 
 
         a_rows = reuse.tile([P, PACK, J], F32, name="a_rows", offset=0)
-        for t in range(PACK):
+        def a_product(bank, t, slots):
             cols = slice(t * P, (t + 1) * P)
-            a_bank = psum.tile([P, J], F32, name="a_bank%d" % t)
             nc.tensor.matmul_mx(
-                out=a_bank[:], lhsT=w_codes[:, cols].bitcast(FP8X4), lhsT_scale=ww_sc[QUADS:P, cols],
-                rhs=xc_codes[:].bitcast(FP8X4), rhs_scale=xc_sc[:], start=True, stop=True,
+                out=bank, lhsT=w_codes[:, cols].bitcast(FP8X4), lhsT_scale=w_sc[:, cols],
+                rhs=xc_codes[:, slots].bitcast(FP8X4), rhs_scale=xc_sc[:, slots], start=True, stop=True,
             )
-            nc.scalar.copy(out=a_rows[:, t, :], in_=a_bank[:])
+
+        for t, first, last in ((1, 0, J // 2), (0, 0, J), (1, J // 2, J)):
+            slots = slice(first, last)
+            a_bank = psum.tile([P, last - first], F32, name="a_bank%d_%d" % (t, first))
+            a_product(a_bank[:], t, slots)
+            nc.scalar.copy(out=a_rows[:, t, slots], in_=a_bank[:])
+            nc.vector.tensor_copy(out=boards[t][:].indirect(list_put[:, first // 16 : last // 16]), in_=a_rows[:, t, slots])
+        a_bank = psum.tile([P, 2, J], F32, name="a_bank23")
+        for t in (2, 3):
+            a_product(a_bank[:, t - 2, :], t, slice(0, J))
+        nc.scalar.copy(out=a_rows[:, 2:4, :], in_=a_bank[:])
+        for t in (2, 3):
             nc.vector.tensor_copy(out=boards[t][:].indirect(list_put[:]), in_=a_rows[:, t, :])
+
+        w2_codes = keep.tile([P, 2 * R], U8, name="w2_codes", align_bytes=64)
+        nc.scalar.copy(
+            out=w2_codes[:].bitcast(U16).rearrange("p (t m) -> p t m", t=PACK),
+            in_=w2_raw[:].bitcast(U16).rearrange("p (m t) -> p t m", t=PACK),
+        )
 
         b_banks = [psum.tile([P, 2, J], F32, name="b_bank%d" % u) for u in range(2)]
         for t in range(PACK):
             nc.tensor.matmul_mx(
                 out=b_banks[t // 2][:, t % 2, :],
-                lhsT=w2_codes[:, 2 * t * P : 2 * (t + 1) * P].bitcast(FP4X4), lhsT_scale=ww_sc[:, t * P : (t + 1) * P],
+                lhsT=w2_codes[:, 2 * t * P : 2 * (t + 1) * P].bitcast(FP4X4), lhsT_scale=w2_sc[:, t * P : (t + 1) * P],
                 rhs=xo_codes[:].bitcast(FP8X4), rhs_scale=xo_sc[:], start=True, stop=True,
             )
 

from contextlib import ExitStack

import concourse.mybir as mybir

F32 = mybir.dt.float32
BF16 = mybir.dt.bfloat16
I32 = mybir.dt.int32
U32 = mybir.dt.uint32
U16 = mybir.dt.uint16
U8 = mybir.dt.uint8
FP8X4 = mybir.dt.float8_e4m3fn_x4
FP4X4 = mybir.dt.float4_e2m1fn_x4
COPY = mybir.ActivationFunctionType.Copy
ADD = mybir.AluOpType.add
MAX = mybir.AluOpType.max

P = 128
PACK = 4
QUADS = 4
K, J, R, T, M, O, C, N = 512, 256, 512, 512, 1024, 128, 512, 256
FLOPS = 2 * K * R * J + 2 * K * R * J + 2 * R * N * O


def tile_picked_twobooks_plain_two_answered_codes_plain_kernel(
    tc, ta, tb, ga, gb, w_words, w_scales, xo_words, xo_scales, w2_words, w2_scales,
    sa, sb, va, ea, offs, offs2, offs3, offs4, offs5, offs6, offs7, out,
):
    nc = tc.nc
    with ExitStack() as ctx:
        lists = ctx.enter_context(tc.tile_pool(name="lists", bufs=1))
        keep = ctx.enter_context(tc.tile_pool(name="keep", bufs=1))
        reuse = ctx.enter_context(tc.tile_pool(name="reuse", bufs=1))
        early = ctx.enter_context(tc.tile_pool(name="early", bufs=1))
        psum = ctx.enter_context(tc.psum_pool(name="psum", bufs=1))

        def load_list(src, name):
            tile = lists.tile([P, src.shape[1]], U16, name=name)
            nc.sync.dma_start(tile[:], src)
            return tile

        def load_factor(src, name, queue, tag=None):
            tile = keep.tile([P, PACK], F32, name=name, tag=tag or name, align_bytes=64)
            queue.dma_start(out=tile[:], in_=src.rearrange("(p t) o -> p (t o)", t=PACK))
            return tile

        def load_plane(src, t, name):
            tile = keep.tile([P, T], F32, name=name, align_bytes=64)
            nc.sync.dma_start(out=tile[:], in_=src.rearrange("(p t) c -> p t c", t=PACK)[:, t, :])
            return tile

        def load_words(src, name):
            tile = keep.tile([P, src.shape[1]], I32, name=name)
            nc.sync.dma_start(out=tile[:], in_=src)
            return tile

        def place_scale_rows(src, name):
            plane = keep.tile([P, src.shape[1]], U8, name=name, align_bytes=64)
            nc.vector.memset(plane[:].bitcast(I32), 0)
            for r in range(QUADS):
                nc.sync.dma_start(out=plane[r:P:32, :].bitcast(I32), in_=src[8 * r : P : 32, :].bitcast(I32))
            return plane

        def deal_bytes(dst, src):
            nc.vector.tensor_copy(out=dst[:].rearrange("p (t m) -> p t m", t=PACK), in_=src[:].rearrange("p (m t) -> p t m", t=PACK))

        def interleave(copy, dst, src):
            copy(out=dst.rearrange("p (c i) t -> p c t i", i=4), in_=src.rearrange("p t (c i) -> p c t i", i=4))

        def dealt(ap):
            return ap.rearrange("p (t m) -> p m t", t=PACK)

        def plain(ap):
            return ap.rearrange("p (m t) -> p m t", t=PACK)

        xo_rows = early.tile([P, M], U8, name="xo_rows", offset=0)
        nc.vector.memset(xo_rows[:].bitcast(I32), 0)
        w2_rows = early.tile([P, R], U8, name="w2_rows", offset=M)
        nc.vector.memset(w2_rows[:].bitcast(I32), 0)
        w_stage = keep.tile([QUADS, QUADS, R // 4], I32, name="w_stage")
        ta_rows = [load_plane(ta, 0, "ta0")]
        list_a = load_list(offs, "list_a")
        ga_col = load_factor(ga, "ga_col", nc.scalar)
        gb_col = load_factor(gb, "gb_col", nc.scalar)
        nc.sync.dma_start(out=w_stage[:], in_=w_scales[0].bitcast(I32).rearrange("(q r) c -> r q c", r=QUADS))
        ta_rows.append(load_plane(ta, 1, "ta1"))
        list_xo = load_list(offs3, "list_xo")
        ta_rows.append(load_plane(ta, 2, "ta2"))
        nc.sync.dma_start(out=xo_rows[0:P:8, :].bitcast(I32), in_=xo_scales[0].bitcast(I32))
        nc.sync.dma_start(out=w2_rows[0:P:8, :].bitcast(I32), in_=w2_scales[0].bitcast(I32))
        ta_rows.append(load_plane(ta, 3, "ta3"))
        list_b = load_list(offs2, "list_b")
        tb_rows = [load_plane(tb, t, "tb%d" % t) for t in range(PACK)]
        w_raw = load_words(w_words[0].rearrange("p n t -> p (n t)").bitcast(I32), "w_raw")
        xo_raw = load_words(xo_words[0].rearrange("p n t -> p (n t)").bitcast(I32), "xo_raw")
        list_put = load_list(offs4, "list_put")
        w2_raw = load_words(w2_words[0].bitcast(I32), "w2_raw")
        list_va = load_list(offs7, "list_va")
        ea_col = load_factor(ea, "ea_col", nc.sync, tag="va4")
        va_rows = [load_plane(va, t, "va%d" % t) for t in range(2)]
        list_board = load_list(offs5, "list_board")
        sa_col = load_factor(sa, "sa_col", nc.sync, tag="sa_then_hid")
        va_rows.extend(load_plane(va, t, "va%d" % t) for t in range(2, PACK))
        list_slot = load_list(offs6, "list_slot")
        sb_col = load_factor(sb, "sb_col", nc.sync)

        def cleared_board(t, tag):
            board = keep.tile([P, C], F32, name="board%d" % t, tag=tag)
            nc.vector.memset(board[:], 0.0)
            return board

        boards = [cleared_board(t, "board%d" % t) for t in range(PACK)]

        w_spread = early.tile([P, R], U8, name="w_spread", offset=M + R)
        nc.vector.memset(w_spread[:].bitcast(I32), 0)
        for q in range(QUADS):
            nc.vector.tensor_copy(out=w_spread[32 * q : 32 * q + QUADS, :].bitcast(I32), in_=w_stage[:, q, :])
        w_sc = keep.tile([P, R], U8, name="w_sc", align_bytes=64)
        deal_bytes(w_sc, w_spread)
        xo_picked = keep.tile([P, J], U8, name="xo_picked")
        nc.vector.tensor_copy(out=xo_picked[:], in_=xo_rows[:].indirect(list_xo[:]))
        xo_sc = place_scale_rows(xo_picked, "xo_sc")
        w2_dealt = keep.tile([P, R], U8, name="w2_dealt")
        deal_bytes(w2_dealt, w2_rows)
        w2_sc = place_scale_rows(w2_dealt, "w2_sc")

        xa = keep.tile([P, PACK, J], F32, name="xa")
        xb = keep.tile([P, PACK, J], F32, name="xb")
        xc = early.tile([P, J, PACK], BF16, name="xc", offset=0, align_bytes=64)

        def add_pair(u, cols):
            nc.vector.tensor_tensor(
                out=xc[:, cols, 2 * u : 2 * u + 2],
                in0=xa[:, 2 * u : 2 * u + 2, cols].rearrange("p t j -> p j t"),
                in1=xb[:, 2 * u : 2 * u + 2, cols].rearrange("p t j -> p j t"),
                op=ADD,
            )

        for t in range(PACK):
            nc.scalar.activation(out=xa[:, t, :], in_=ta_rows[t][:].indirect(list_a[:]), func=COPY, scale=ga_col[:, t : t + 1])
        for t in range(PACK - 1):
            nc.scalar.activation(out=xb[:, t, :], in_=tb_rows[t][:].indirect(list_b[:]), func=COPY, scale=gb_col[:, t : t + 1])
        add_pair(0, slice(0, J))
        for h in range(2):
            cols = slice(h * J // 2, (h + 1) * J // 2)
            nc.scalar.activation(
                out=xb[:, PACK - 1, cols],
                in_=tb_rows[PACK - 1][:].indirect(list_b[:, h * J // 32 : (h + 1) * J // 32]),
                func=COPY,
                scale=gb_col[:, PACK - 1 : PACK],
            )
            add_pair(1, cols)

        w_codes = keep.tile([P, R], U32, name="w_codes", align_bytes=64)
        nc.scalar.copy(out=dealt(w_codes[:]), in_=plain(w_raw[:].bitcast(U32)))

        xc_codes = keep.tile([P, J], U32, name="xc_codes", align_bytes=64)
        xc_sc = keep.tile([P, J], U8, name="xc_sc", align_bytes=64)
        for h in range(2):
            cols = slice(h * J // 2, (h + 1) * J // 2)
            nc.vector.quantize_mx(out=xc_codes[:, cols].bitcast(FP8X4), scales=xc_sc[:, cols], in_=xc[:, cols, :].rearrange("p j t -> p (j t)"))

        xo_codes = keep.tile([P, J], U32, name="xo_codes", align_bytes=64)
        nc.vector.tensor_copy(out=xo_codes[:], in_=xo_raw[:].bitcast(U32).indirect(list_xo[:]))


        a_rows = reuse.tile([P, PACK, J], F32, name="a_rows", offset=0)
        def a_product(bank, t, slots):
            cols = slice(t * P, (t + 1) * P)
            nc.tensor.matmul_mx(
                out=bank, lhsT=w_codes[:, cols].bitcast(FP8X4), lhsT_scale=w_sc[:, cols],
                rhs=xc_codes[:, slots].bitcast(FP8X4), rhs_scale=xc_sc[:, slots], start=True, stop=True,
            )

        for t, first, last in ((1, 0, J // 2), (0, 0, J), (1, J // 2, J)):
            slots = slice(first, last)
            a_bank = psum.tile([P, last - first], F32, name="a_bank%d_%d" % (t, first))
            a_product(a_bank[:], t, slots)
            nc.scalar.copy(out=a_rows[:, t, slots], in_=a_bank[:])
            nc.vector.tensor_copy(out=boards[t][:].indirect(list_put[:, first // 16 : last // 16]), in_=a_rows[:, t, slots])
        a_bank = psum.tile([P, 2, J], F32, name="a_bank23")
        for t in (2, 3):
            a_product(a_bank[:, t - 2, :], t, slice(0, J))
        nc.scalar.copy(out=a_rows[:, 2:4, :], in_=a_bank[:])
        for t in (2, 3):
            nc.vector.tensor_copy(out=boards[t][:].indirect(list_put[:]), in_=a_rows[:, t, :])

        w2_codes = keep.tile([P, 2 * R], U8, name="w2_codes", align_bytes=64)
        nc.scalar.copy(
            out=w2_codes[:].bitcast(U16).rearrange("p (t m) -> p t m", t=PACK),
            in_=w2_raw[:].bitcast(U16).rearrange("p (m t) -> p t m", t=PACK),
        )

        b_banks = [psum.tile([P, 2, J], F32, name="b_bank%d" % u) for u in range(2)]
        for t in range(PACK):
            nc.tensor.matmul_mx(
                out=b_banks[t // 2][:, t % 2, :],
                lhsT=w2_codes[:, 2 * t * P : 2 * (t + 1) * P].bitcast(FP4X4), lhsT_scale=w2_sc[:, t * P : (t + 1) * P],
                rhs=xo_codes[:].bitcast(FP8X4), rhs_scale=xo_sc[:], start=True, stop=True,
            )

        vc_rows = keep.tile([P, PACK, N], BF16, name="vc_rows")
        for t in range(PACK):
            nc.scalar.activation(out=vc_rows[:, t, :], in_=va_rows[t][:].indirect(list_va[:]), func=COPY, scale=ea_col[:, t : t + 1])

        vc_lo = keep.tile([P, P, PACK], BF16, name="vc_lo", align_bytes=64)
        interleave(nc.scalar.copy, vc_lo[:], vc_rows[:, :, 0:P])

        answers = []
        for t in range(PACK):
            read = keep.tile([P, J], F32, name="read%d" % t, tag="va%d" % (t + 1), align_bytes=64)
            nc.scalar.activation(out=read[:], in_=boards[t][:].indirect(list_board[:]), func=COPY, scale=sa_col[:, t : t + 1])
            answer = reuse.tile([P, J], F32, name="answer%d" % t, offset=4 * J * t)
            nc.vector.tensor_tensor(out=answer[:], in0=read[:], in1=b_banks[t // 2][:, t % 2, :], op=MAX)
            answers.append(answer)
        vc_hi = keep.tile([P, P, PACK], BF16, name="vc_hi", tag="va1", align_bytes=64)
        interleave(nc.vector.tensor_copy, vc_hi[:], vc_rows[:, :, P:N])
        vc_codes = keep.tile([P, N], U32, name="vc_codes", align_bytes=64)
        vc_sc = keep.tile([P, N], U8, name="vc_sc", tag="va2", align_bytes=64)
        for h, half in enumerate((vc_lo, vc_hi)):
            cols = slice(h * P, (h + 1) * P)
            nc.vector.quantize_mx(out=vc_codes[:, cols].bitcast(FP8X4), scales=vc_sc[:, cols], in_=half[:].rearrange("p n t -> p (n t)"))
        hid_rows = keep.tile([P, PACK, O], BF16, name="hid_rows", tag="sa_then_hid", align_bytes=64)
        for t in range(PACK):
            nc.scalar.activation(out=hid_rows[:, t, :], in_=answers[t][:].indirect(list_slot[:]), func=COPY, scale=sb_col[:, t : t + 1])
        hid = keep.tile([P, O, PACK], BF16, name="hid", align_bytes=64)
        for u in range(2):
            pair = slice(2 * u, 2 * u + 2)
            nc.vector.tensor_copy(out=hid[:, :, pair], in_=hid_rows[:, pair, :].rearrange("p t o -> p o t"))
        hid_codes = keep.tile([P, O], U32, name="hid_codes", align_bytes=64)
        hid_sc = keep.tile([P, O], U8, name="hid_sc", align_bytes=64)
        nc.vector.quantize_mx(out=hid_codes[:].bitcast(FP8X4), scales=hid_sc[:], in_=hid[:].rearrange("p o t -> p (o t)"))

        for h in range(2):
            cols = slice(h * P, (h + 1) * P)
            y_bank = psum.tile([P, O], F32, name="y_bank%d" % h)
            nc.tensor.matmul_mx(
                out=y_bank[:], lhsT=vc_codes[:, cols].bitcast(FP8X4), lhsT_scale=vc_sc[:, cols],
                rhs=hid_codes[:].bitcast(FP8X4), rhs_scale=hid_sc[:], start=True, stop=True,
            )
            y = keep.tile([P, O], F32, name="y%d" % h)
            if h == 0:
                nc.vector.tensor_copy(out=y[:], in_=y_bank[:])
                nc.sync.dma_start(out=out[cols, :], in_=y[:])
            else:
                nc.scalar.copy(out=y[:], in_=y_bank[:])
                nc.scalar.dma_start(out=out[cols, :], in_=y[:])
